import numpy as np
import ml_dtypes


def mxq(x, axis, fmt="e4m3"):
    dtype, down = {"e4m3": (ml_dtypes.float8_e4m3fn, 7), "e5m2": (ml_dtypes.float8_e5m2, 14)}[fmt]
    v = np.moveaxis(np.asarray(x, np.float32).astype(ml_dtypes.bfloat16).astype(np.float64), axis, -1)
    blocks = v.reshape(v.shape[:-1] + (-1, 32))
    amax = np.abs(blocks).max(-1, keepdims=True)
    byte = np.maximum(np.where(amax > 0, np.frexp(amax)[1] - 1 + 127, 0) - down, 1)
    scale = np.exp2(byte - 127.0)
    codes = (blocks / scale).astype(np.float32).astype(dtype).astype(np.float64)
    return np.moveaxis((codes * scale).reshape(v.shape), -1, axis)


WIDE = False


def mx_kscale(k):
    if not WIDE:
        return np.ones(k)
    levels = np.array([10, -10, 5, -5, 0])
    if k % 512:
        return np.exp2(np.random.permutation(np.resize(levels, k // 32))).repeat(32)
    a = np.empty((k // 512, 16))
    for p in range(k // 512):
        a[p, :8] = np.random.permutation(np.resize(levels, 8))
        for g in range(8):
            far = levels[np.abs(levels - a[p, g]) >= 10]
            a[p, g + 8] = far[np.random.randint(len(far))]
    return np.exp2(a.ravel()).repeat(32)


def f64(x):
    return np.asarray(x).astype(np.float64)


def striped(idx):
    return np.tile(idx.reshape(-1, 16).T, (8, 1)).astype(np.uint16)


def unstriped(offs):
    return offs[:16].T.reshape(-1).astype(np.int64)


E2M1 = np.array([0.0, 0.5, 1.0, 1.5, 2.0, 3.0, 4.0, 6.0, -0.0, -0.5, -1.0, -1.5, -2.0, -3.0, -4.0, -6.0])


def pack_weight(w, fmt):
    k, n = w.shape
    w = f64(np.asarray(w, np.float32).astype(ml_dtypes.bfloat16)).reshape(k // 32, 32, n)
    amax = np.abs(w).max(1)
    if fmt == "e4m3":
        byte = np.frexp(amax)[1] - 1 + 127 - 7
    else:
        mant, ex = np.frexp(amax / 6.0)
        byte = np.where(mant > 0.5, ex, ex - 1) + 127
    byte = np.clip(np.where(amax > 0, byte, 1), 1, 254)
    scaled = (w * np.exp2(127.0 - byte)[:, None, :]).reshape(k, n).astype(np.float32)
    by_word = np.ascontiguousarray(scaled.reshape(k // 512, 128, 4, n).transpose(0, 1, 3, 2))
    if fmt == "e4m3":
        words = by_word.astype(ml_dtypes.float8_e4m3fn).view(np.uint8)
    else:
        c = by_word.astype(ml_dtypes.float4_e2m1fn).view(np.uint8) & 0xF
        words = (c[..., 0::2] | (c[..., 1::2] << 4)).reshape(k // 512, 128, 2 * n)
    return np.ascontiguousarray(words), np.ascontiguousarray(byte.astype(np.uint8).reshape(k // 512, 16, n))


def unpack_weight(words, scales, fmt):
    g, _, n = scales.shape
    words = np.ascontiguousarray(words).reshape(g, 128, n, -1)
    if fmt == "e4m3":
        vals = words.view(ml_dtypes.float8_e4m3fn).astype(np.float64)
    else:
        nib = np.empty((g, 128, n, 4), np.uint8)
        nib[..., 0::2] = words & 0xF
        nib[..., 1::2] = words >> 4
        vals = E2M1[nib]
    vals = vals * np.repeat(np.exp2(scales.astype(np.float64) - 127.0), 8, axis=1)[..., None]
    return vals.transpose(0, 1, 3, 2).reshape(g * 512, n)


def gelu(v):
    return 0.5 * v * (1.0 + np.tanh(np.sqrt(2.0 / np.pi) * (v + 0.044715 * v**3)))


K, T, S, H, T3, S2, T2, P = 1536, 2048, 512, 1024, 2048, 512, 1024, 512

def setup_inputs():
    n = np.random.standard_normal
    s = mx_kscale(K)[:, None]
    u = mx_kscale(H)[:, None]
    tab_words, tab_scales = pack_weight(n((K, T)) * s, "e4m3")
    tab2_words, tab2_scales = pack_weight(n((H, T3)) / np.sqrt(H) / u, "e4m3")
    w4_words, w4_scales = pack_weight(0.4 * n((K, H)) / np.sqrt(K) / s, "e2m1")
    return {
        "tab_words": tab_words, "tab_scales": tab_scales,
        "offs": striped(np.random.permutation(T)[:S]),
        "w1": (n((K, H)) / np.sqrt(K) / s * u.T).astype(np.float32),
        "w4_words": w4_words, "w4_scales": w4_scales,
        "bias": np.random.uniform(-0.9, 0.9, H).astype(np.float32),
        "resid": (0.6 * n((H, S)) * u).astype(np.float32),
        "page0": (n((H, T2)) * u).astype(np.float32),
        "wgs": np.exp(0.3 * n((128, S))).astype(np.float32),
        "tab2_words": tab2_words, "tab2_scales": tab2_scales,
        "offs2": striped(np.random.permutation(T3)[:S2]),
        "offs3": striped(np.random.permutation(T2)[:S]),
        "pos1": striped(np.random.permutation(T2)[:P]),
        "pos2": striped(np.random.permutation(T2)[:P]),
        "acc": n((S2, P)).astype(np.float32),
    }

def reference(tab_words, tab_scales, offs, w1, w4_words, w4_scales, bias, resid, page0, wgs, tab2_words, tab2_scales, offs2, offs3, pos1, pos2, acc):
    v = unpack_weight(tab_words, tab_scales, "e4m3")[:, unstriped(offs)]
    v2 = unpack_weight(tab2_words, tab2_scales, "e4m3")[:, unstriped(offs2)]
    w4 = unpack_weight(w4_words, w4_scales, "e2m1")
    a = mxq(f64(w1), 0, "e4m3").T @ v
    d = w4.T @ v
    h = a * np.cos(d + f64(bias)[:, None]) + f64(resid)
    page = f64(page0).copy()
    page[:, unstriped(offs3)] = np.tile(f64(wgs), (H // 128, 1)) * h
    e = v2.T @ mxq(page, 0, "e4m3")
    rival = np.minimum(e[:, unstriped(pos1)], e[:, unstriped(pos2)])
    return np.minimum(rival, f64(acc))

@@ -1,0 +1,281 @@
+import math
+from contextlib import ExitStack
+
+import concourse.mybir as mybir
+from concourse.masks import make_identity
+
+K, T, S, H, T3, S2, T2, NP = 1536, 2048, 512, 1024, 2048, 512, 1024, 512
+FLOPS = 2 * (2 * K * H * S + H * S2 * T2)
+
+F32 = mybir.dt.float32
+BF16 = mybir.dt.bfloat16
+I32 = mybir.dt.int32
+U32 = mybir.dt.uint32
+U16 = mybir.dt.uint16
+U8 = mybir.dt.uint8
+FP8X4 = mybir.dt.float8_e4m3fn_x4
+FP4X4 = mybir.dt.float4_e2m1fn_x4
+ALU = mybir.AluOpType
+ACT = mybir.ActivationFunctionType
+
+P = 128
+PACK = 4
+KP = P * PACK
+K_PASSES = K // KP
+R_PASSES = H // KP
+R_TILES = H // P
+M_TILES = S2 // P
+CHUNK = 256
+CHUNKS = H // CHUNK
+BANK = 512
+HALVES = T2 // BANK
+
+
+def tile_list_gazetteer_rival_scores_kernel(
+    tc, tab_words, tab_scales, offs, w1, w4_words, w4_scales, bias, resid, page0, wgs,
+    tab2_words, tab2_scales, offs2, offs3, pos1, pos2, acc, out,
+):
+    nc = tc.nc
+    with ExitStack() as ctx:
+        keep = ctx.enter_context(tc.tile_pool(name="keep", bufs=1))
+        work = ctx.enter_context(tc.tile_pool(name="work", bufs=1))
+        psum = ctx.enter_context(tc.psum_pool(name="psum", bufs=1))
+
+        def bank(tag):
+            return psum.tile([P, BANK], F32, name=tag, tag=tag)
+
+        def load_list(src, name):
+            t = keep.tile([P, S // 16], U16, name=name)
+            nc.sync.dma_start(t[:], src)
+            return t
+
+        def load_scale_rows(src, passes, width, name):
+            t = keep.tile([P, passes, width], U8, name=name, align_bytes=64)
+            words = t[:].bitcast(I32)
+            nc.vector.memset(words, 0)
+            rows = src.bitcast(I32).rearrange("a (q r) w -> r q a w", r=4)
+            for r in range(4):
+                nc.gpsimd.dma_start(words[r:P:32], rows[r])
+            return t
+
+        def load_words(src, name):
+            t = work.tile([P, T], U32, name=name, tag=name)
+            nc.sync.dma_start(t[:].bitcast(I32), src.rearrange("p t i -> p (t i)").bitcast(I32))
+            return t
+
+        def gather(window, lst, dtype, name):
+            t = keep.tile([P, S], dtype, name=name, align_bytes=64)
+            nc.vector.tensor_copy(t[:], window.indirect(lst[:]))
+            return t
+
+        tab_sc = load_scale_rows(tab_scales, K_PASSES, T, "tab_sc")
+        w4_sc = load_scale_rows(w4_scales, K_PASSES, H, "w4_sc")
+        ident = keep.tile([P, P], F32, name="ident")
+        make_identity(nc, ident[:])
+        half_pi = keep.tile([P, 1], F32, name="half_pi")
+        zero = keep.tile([P, 1], F32, name="zero")
+        nc.vector.memset(zero[:], 0.0)
+        nc.vector.tensor_scalar_add(half_pi[:], zero[:], math.pi / 2)
+        bias_rows = keep.tile([P, P], F32, name="bias_rows")
+        nc.vector.memset(bias_rows[:], 0.0)
+        tab2_sc = keep.tile([P, T3], U8, name="tab2_sc", align_bytes=64)
+        nc.vector.memset(tab2_sc[:].bitcast(I32), 0)
+        for quad in range(4):
+            nc.gpsimd.dma_start(
+                tab2_sc[:].bitcast(I32)[32 * quad : 32 * quad + 4 * R_PASSES, :],
+                tab2_scales.bitcast(I32)[:, 4 * quad : 4 * quad + 4, :],
+            )
+
+        l_offs = load_list(offs, "l_offs")
+
+        w1_codes, w1_sc = {}, {}
+
+        def load_w1(ch):
+            raws = []
+            for a in range(K_PASSES):
+                raw = work.tile([P, PACK, CHUNK], F32, name="w1_raw", tag="w1_raw", bufs=6)
+                nc.sync.dma_start(
+                    raw[:],
+                    w1[a * KP : (a + 1) * KP, ch * CHUNK : (ch + 1) * CHUNK].rearrange("(p j) c -> p j c", j=PACK),
+                )
+                raws.append(raw)
+            return raws
+
+        def quantise_w1(ch, raws):
+            codes = keep.tile([P, K_PASSES, CHUNK], U32, name=f"w1_codes{ch}", align_bytes=64)
+            sc = keep.tile([P, K_PASSES, CHUNK], U8, name=f"w1_sc{ch}", align_bytes=64)
+            for a in range(K_PASSES):
+                tag = "w1_last" if a == K_PASSES - 1 else f"w1_bf{a}"
+                grouped = work.tile([P, CHUNK, PACK], BF16, name=tag, tag=tag, align_bytes=64)
+                nc.scalar.copy(
+                    grouped[:].rearrange("p (c i) t -> p c t i", i=4),
+                    raws[a][:].rearrange("p t (c i) -> p c t i", i=4),
+                )
+                nc.vector.quantize_mx(
+                    out=codes[:, a, :].bitcast(FP8X4), scales=sc[:, a, :],
+                    in_=grouped[:].rearrange("p c t -> p (c t)"),
+                )
+            w1_codes[ch], w1_sc[ch] = codes, sc
+
+        def load_w4(c0, c1, name):
+            t = keep.tile([P, K_PASSES, 2 * (c1 - c0)], U8, name=name, align_bytes=64)
+            nc.sync.dma_start(
+                t[:].bitcast(I32),
+                w4_words.bitcast(I32)[:, :, c0 // 2 : c1 // 2].rearrange("a p w -> p a w"),
+            )
+            return t
+
+        def load_resid(ch):
+            t = keep.tile([P, 2, S], F32, name=f"resid{ch}")
+            nc.sync.dma_start(t[:], resid[ch * CHUNK : (ch + 1) * CHUNK, :].rearrange("(c q) j -> q c j", q=P))
+            return t
+
+        def load_page(i):
+            t = keep.tile([P, T2], F32, name=f"page{i}")
+            nc.sync.dma_start(t[:], page0[i * P : (i + 1) * P, :])
+            return t
+
+        raws = {0: load_w1(0)}
+        w4_first = load_w4(0, CHUNK, "w4_first")
+        tab_w = [load_words(tab_words[a], f"tab_w{a}") for a in range(K_PASSES)]
+        l_offs3 = load_list(offs3, "l_offs3")
+        nc.sync.dma_start(bias_rows[0:R_TILES, :], bias.rearrange("(c q) -> c q", q=P))
+        resids = {0: load_resid(0)}
+        wgs_sb = work.tile([P, S], F32, name="wgs_sb", tag="wgs_sb", align_bytes=64)
+        nc.sync.dma_start(wgs_sb[:], wgs)
+        pages = {0: load_page(0)}
+        raws[1] = load_w1(1)
+        pages[1] = load_page(1)
+        w4_rest = load_w4(CHUNK, H, "w4_rest")
+
+        bias_ps = bank("t0")
+        nc.tensor.transpose(bias_ps[:, 0:P], bias_rows[:], ident[:])
+        bias_sb = keep.tile([P, R_TILES], F32, name="bias_sb")
+        nc.scalar.copy(bias_sb[:], bias_ps[:, 0:R_TILES])
+
+        v_sc = [gather(tab_sc[:, a, :], l_offs, U8, f"v_sc{a}") for a in range(K_PASSES)]
+        quantise_w1(0, raws[0])
+        v_w = [gather(tab_w[a][:], l_offs, U32, f"v_w{a}") for a in range(K_PASSES)]
+
+        def features(i):
+            ch, c = divmod(i, CHUNK // P)
+            d_ps = bank(f"d{i % 2}")
+            a_ps = bank(f"a{i % 2}")
+            w4_t, c0 = (w4_first, i * P) if ch == 0 else (w4_rest, i * P - CHUNK)
+            for a in range(K_PASSES):
+                nc.tensor.matmul_mx(
+                    out=d_ps[:], lhsT=w4_t[:, a, 2 * c0 : 2 * (c0 + P)].bitcast(FP4X4),
+                    lhsT_scale=w4_sc[:, a, i * P : (i + 1) * P],
+                    rhs=v_w[a][:].bitcast(FP8X4), rhs_scale=v_sc[a][:],
+                    start=(a == 0), stop=(a == K_PASSES - 1),
+                )
+            for a in range(K_PASSES):
+                nc.tensor.matmul_mx(
+                    out=a_ps[:], lhsT=w1_codes[ch][:, a, c * P : (c + 1) * P].bitcast(FP8X4),
+                    lhsT_scale=w1_sc[ch][:, a, c * P : (c + 1) * P],
+                    rhs=v_w[a][:].bitcast(FP8X4), rhs_scale=v_sc[a][:],
+                    start=(a == 0), stop=(a == K_PASSES - 1),
+                )
+            mag = work.tile([P, S], F32, name="mag", tag="mag", bufs=2)
+            nc.scalar.activation(mag[:], d_ps[:], ACT.Abs, bias=bias_sb[:, i : i + 1])
+            cosine = work.tile([P, S], F32, name="cosine", tag="cosine", bufs=2)
+            nc.scalar.activation(cosine[:], mag[:], ACT.Sin, bias=half_pi[:], scale=-1.0)
+            prod = work.tile([P, S], F32, name="prod", tag="prod", bufs=2)
+            nc.vector.tensor_tensor(prod[:], a_ps[:], cosine[:], ALU.mult)
+            tag = {4: "h_mid", 7: "h_end"}.get(i, "w1_last" if i % 2 else "h")
+            h = work.tile([P, S], F32, name=tag, tag=tag, align_bytes=64)
+            nc.vector.tensor_tensor(h[:], prod[:], resids[ch][:, c, :], ALU.add)
+            return h
+
+        turned = {}
+
+        def place(i, h):
+            nc.vector.tensor_tensor(pages[i][:].indirect(l_offs3[:]), h[:], wgs_sb[:], ALU.mult)
+
+        def turn(i):
+            b, c = divmod(i, PACK)
+            for half, tag in enumerate((f"d{(i + 1) % 2}", f"a{(i + 1) % 2}")):
+                if c == 0:
+                    turned[b, half] = work.tile([P, 4, 2, 4, 64], BF16, name=f"turned{b}{half}")
+                ps = bank(tag)
+                for k in range(4):
+                    n0 = half * BANK + k * P
+                    nc.tensor.transpose(ps[:, k * P : (k + 1) * P], pages[i][:, n0 : n0 + P], ident[:])
+                nc.scalar.copy(
+                    turned[b, half][:, :, :, c, :].rearrange("n k u (p e) -> n k u p e", e=2),
+                    ps[:].rearrange("n (k p u e) -> n k u p e", k=4, u=2, e=2),
+                )
+
+        page_codes, page_sc = {}, {}
+
+        def quantise_page(b):
+            tag = "h_mid" if b == 0 else "page_codes"
+            both = work.tile([P, HALVES, BANK], U32, name=tag, tag=tag, align_bytes=64)
+            for half in range(HALVES):
+                words = turned[b, half][:].rearrange("n k u c w -> n (k u c w)").bitcast(F32)
+                grouped = work.tile([P, BANK * PACK], BF16, name="page_bf", tag="page_bf", bufs=2, align_bytes=64)
+                pairs = grouped[:].bitcast(F32).rearrange("p (g k n u) -> p g k n u", g=2, k=2, u=2)
+                for g in range(2):
+                    ps = bank(f"t{2 * half + g}")
+                    for ku in range(4):
+                        w0 = (4 * g + ku) * P
+                        nc.tensor.transpose(ps[:, ku * P : (ku + 1) * P], words[:, w0 : w0 + P], ident[:])
+                    nc.scalar.copy(pairs[:, g], ps[:].rearrange("p (k u n) -> p k n u", k=2, u=2))
+                codes = both[:, half, :]
+                sc = keep.tile([P, BANK], U8, name=f"page_sc{b}{half}", align_bytes=64)
+                nc.vector.quantize_mx(out=codes.bitcast(FP8X4), scales=sc[:], in_=grouped[:])
+                page_codes[b, half], page_sc[b, half] = codes, sc
+
+        h_now = features(0)
+        for i in range(R_TILES):
+            ch = i // 2
+            if i % 2 == 0 and ch + 1 < CHUNKS:
+                if ch > 0:
+                    raws[ch + 1] = load_w1(ch + 1)
+                    pages[i + 1] = load_page(i + 1)
+                resids[ch + 1] = load_resid(ch + 1)
+                pages[i + 2] = load_page(i + 2)
+                quantise_w1(ch + 1, raws[ch + 1])
+            if i == R_TILES - 2:
+                l_offs2 = load_list(offs2, "l_offs2")
+                tab2_w = [load_words(tab2_words[b], f"tab_w{b}") for b in range(R_PASSES)]
+                pages[i + 1] = load_page(i + 1)
+            place(i, h_now)
+            if i + 1 < R_TILES:
+                h_now = features(i + 1)
+            turn(i)
+            if i == PACK:
+                quantise_page(0)
+
+        l_pos1 = load_list(pos1, "l_pos1")
+        l_pos2 = load_list(pos2, "l_pos2")
+        acc_sb = keep.tile([P, M_TILES, NP], F32, name="acc_sb")
+        nc.sync.dma_start(acc_sb[:], acc.rearrange("(m q) j -> q m j", q=P))
+        v2_sc = work.tile([P, S2], U8, name="v2_sc", tag="wgs_sb", align_bytes=64)
+        nc.vector.tensor_copy(v2_sc[:], tab2_sc[:].indirect(l_offs2[:]))
+        v2_w = work.tile([P, R_PASSES, S2], U32, name="v2_w", tag="h_end", align_bytes=64)
+        for b in range(R_PASSES):
+            nc.vector.tensor_copy(v2_w[:, b, :], tab2_w[b][:].indirect(l_offs2[:]))
+        quantise_page(R_PASSES - 1)
+
+        for m in range(M_TILES):
+            cols = slice(m * P, (m + 1) * P)
+            scores = work.tile([P, T2], F32, name="scores", tag="scores", bufs=3)
+            for half in range(HALVES):
+                ps = bank(("d", "a")[half] + str((m + 1) % 2))
+                for b in range(R_PASSES):
+                    nc.tensor.matmul_mx(
+                        out=ps[:], lhsT=v2_w[:, b, cols].bitcast(FP8X4), lhsT_scale=v2_sc[4 * b : P, cols],
+                        rhs=page_codes[b, half].bitcast(FP8X4), rhs_scale=page_sc[b, half][:],
+                        start=(b == 0), stop=(b == R_PASSES - 1),
+                    )
+                nc.scalar.copy(scores[:, half * BANK : (half + 1) * BANK], ps[:])
+            first = work.tile([P, NP], F32, name="first", tag="first", bufs=2)
+            nc.vector.tensor_copy(first[:], scores[:].indirect(l_pos1[:]))
+            second = work.tile([P, NP], F32, name="second", tag="second", bufs=2)
+            nc.vector.tensor_copy(second[:], scores[:].indirect(l_pos2[:]))
+            capped = work.tile([P, NP], F32, name="capped", tag="capped", bufs=2)
+            nc.vector.tensor_tensor(capped[:], first[:], acc_sb[:, m, :], ALU.min)
+            result = work.tile([P, NP], F32, name="result", tag="result", bufs=2)
+            nc.vector.tensor_tensor(result[:], capped[:], second[:], ALU.min)
+            nc.sync.dma_start(out[cols, :], result[:])

@@ -49,14 +49,16 @@ def tile_list_gazetteer_rival_scores_kernel(
             nc.sync.dma_start(t[:], src)
             return t
 
-        def load_scale_rows(src, passes, width, name):
+        def scale_tile(passes, width, name):
             t = keep.tile([P, passes, width], U8, name=name, align_bytes=64)
+            nc.vector.memset(t[:].bitcast(I32), 0)
+            return t
+
+        def load_scale_rows(t, src):
             words = t[:].bitcast(I32)
-            nc.vector.memset(words, 0)
             rows = src.bitcast(I32).rearrange("a (q r) w -> r q a w", r=4)
             for r in range(4):
-                nc.gpsimd.dma_start(words[r:P:32], rows[r])
-            return t
+                nc.sync.dma_start(words[r:P:32], rows[r])
 
         def load_words(src, name):
             t = work.tile([P, T], U32, name=name, tag=name)
@@ -68,23 +70,20 @@ def tile_list_gazetteer_rival_scores_kernel(
             nc.vector.tensor_copy(t[:], window.indirect(lst[:]))
             return t
 
-        tab_sc = load_scale_rows(tab_scales, K_PASSES, T, "tab_sc")
-        w4_sc = load_scale_rows(w4_scales, K_PASSES, H, "w4_sc")
+        tab_sc = scale_tile(K_PASSES, T, "tab_sc")
+        w4_sc = scale_tile(K_PASSES, H, "w4_sc")
         ident = keep.tile([P, P], F32, name="ident")
         make_identity(nc, ident[:])
         half_pi = keep.tile([P, 1], F32, name="half_pi")
         zero = keep.tile([P, 1], F32, name="zero")
         nc.vector.memset(zero[:], 0.0)
         nc.vector.tensor_scalar_add(half_pi[:], zero[:], math.pi / 2)
+        warm = keep.tile([P, 1], F32, name="warm")
+        nc.scalar.activation(warm[:], zero[:], ACT.Sin, bias=zero[:])
         bias_rows = keep.tile([P, P], F32, name="bias_rows")
         nc.vector.memset(bias_rows[:], 0.0)
         tab2_sc = keep.tile([P, T3], U8, name="tab2_sc", align_bytes=64)
         nc.vector.memset(tab2_sc[:].bitcast(I32), 0)
-        for quad in range(4):
-            nc.gpsimd.dma_start(
-                tab2_sc[:].bitcast(I32)[32 * quad : 32 * quad + 4 * R_PASSES, :],
-                tab2_scales.bitcast(I32)[:, 4 * quad : 4 * quad + 4, :],
-            )
 
         l_offs = load_list(offs, "l_offs")
 
@@ -93,7 +92,10 @@ def tile_list_gazetteer_rival_scores_kernel(
         def load_w1(ch):
             raws = []
             for a in range(K_PASSES):
-                raw = work.tile([P, PACK, CHUNK], F32, name="w1_raw", tag="w1_raw", bufs=6)
+                if ch == CHUNKS - 1 and a > 0:
+                    raw = work.tile([P, PACK, CHUNK], F32, name=f"turned0{a - 1}", tag=f"turned0{a - 1}")
+                else:
+                    raw = work.tile([P, PACK, CHUNK], F32, name="w1_raw", tag="w1_raw", bufs=6)
                 nc.sync.dma_start(
                     raw[:],
                     w1[a * KP : (a + 1) * KP, ch * CHUNK : (ch + 1) * CHUNK].rearrange("(p j) c -> p j c", j=PACK),
@@ -102,12 +104,14 @@ def tile_list_gazetteer_rival_scores_kernel(
             return raws
 
         def quantise_w1(ch, raws):
-            codes = keep.tile([P, K_PASSES, CHUNK], U32, name=f"w1_codes{ch}", align_bytes=64)
+            tag = "cos_second" if ch == 1 else f"w1_codes{ch}"
+            codes = work.tile([P, K_PASSES, CHUNK], U32, name=tag, tag=tag, align_bytes=64)
             sc = keep.tile([P, K_PASSES, CHUNK], U8, name=f"w1_sc{ch}", align_bytes=64)
             for a in range(K_PASSES):
-                tag = "w1_last" if a == K_PASSES - 1 else f"w1_bf{a}"
+                tag = f"w1_last{ch % 2}" if a == K_PASSES - 1 else f"w1_bf{a}{ch % 2}"
                 grouped = work.tile([P, CHUNK, PACK], BF16, name=tag, tag=tag, align_bytes=64)
-                nc.scalar.copy(
+                round_copy = nc.vector.tensor_copy if ch == 0 else nc.scalar.copy
+                round_copy(
                     grouped[:].rearrange("p (c i) t -> p c t i", i=4),
                     raws[a][:].rearrange("p t (c i) -> p c t i", i=4),
                 )
@@ -131,15 +135,19 @@ def tile_list_gazetteer_rival_scores_kernel(
             return t
 
         def load_page(i):
-            t = keep.tile([P, T2], F32, name=f"page{i}")
+            t = work.tile([P, T2], F32, name=f"page{i}", tag=f"page{i}", align_bytes=64)
             nc.sync.dma_start(t[:], page0[i * P : (i + 1) * P, :])
             return t
 
-        raws = {0: load_w1(0)}
         w4_first = load_w4(0, CHUNK, "w4_first")
-        tab_w = [load_words(tab_words[a], f"tab_w{a}") for a in range(K_PASSES)]
-        l_offs3 = load_list(offs3, "l_offs3")
+        tab_w = [load_words(tab_words[0], "tab_w0")]
+        load_scale_rows(tab_sc, tab_scales)
+        tab_w.append(load_words(tab_words[1], "tab_w1"))
+        load_scale_rows(w4_sc, w4_scales)
         nc.sync.dma_start(bias_rows[0:R_TILES, :], bias.rearrange("(c q) -> c q", q=P))
+        tab_w.append(load_words(tab_words[2], "tab_w2"))
+        raws = {0: load_w1(0)}
+        l_offs3 = load_list(offs3, "l_offs3")
         resids = {0: load_resid(0)}
         wgs_sb = work.tile([P, S], F32, name="wgs_sb", tag="wgs_sb", align_bytes=64)
         nc.sync.dma_start(wgs_sb[:], wgs)
@@ -147,6 +155,16 @@ def tile_list_gazetteer_rival_scores_kernel(
         raws[1] = load_w1(1)
         pages[1] = load_page(1)
         w4_rest = load_w4(CHUNK, H, "w4_rest")
+        resids[1] = load_resid(1)
+        pages[2] = load_page(2)
+        raws[2] = load_w1(2)
+        pages[3] = load_page(3)
+        raws[3] = load_w1(3)
+        resids[2] = load_resid(2)
+        pages[4] = load_page(4)
+        pages[5] = load_page(5)
+        resids[3] = load_resid(3)
+        pages[6] = load_page(6)
 
         bias_ps = bank("t0")
         nc.tensor.transpose(bias_ps[:, 0:P], bias_rows[:], ident[:])
@@ -154,13 +172,14 @@ def tile_list_gazetteer_rival_scores_kernel(
         nc.scalar.copy(bias_sb[:], bias_ps[:, 0:R_TILES])
 
         v_sc = [gather(tab_sc[:, a, :], l_offs, U8, f"v_sc{a}") for a in range(K_PASSES)]
-        quantise_w1(0, raws[0])
         v_w = [gather(tab_w[a][:], l_offs, U32, f"v_w{a}") for a in range(K_PASSES)]
+        quantise_w1(0, raws[0])
 
         def features(i):
             ch, c = divmod(i, CHUNK // P)
-            d_ps = bank(f"d{i % 2}")
-            a_ps = bank(f"a{i % 2}")
+            side = 0 if i == 1 else i % 2
+            d_ps = bank(f"d{side}")
+            a_ps = bank(f"a{side}")
             w4_t, c0 = (w4_first, i * P) if ch == 0 else (w4_rest, i * P - CHUNK)
             for a in range(K_PASSES):
                 nc.tensor.matmul_mx(
@@ -178,11 +197,21 @@ def tile_list_gazetteer_rival_scores_kernel(
                 )
             mag = work.tile([P, S], F32, name="mag", tag="mag", bufs=2)
             nc.scalar.activation(mag[:], d_ps[:], ACT.Abs, bias=bias_sb[:, i : i + 1])
-            cosine = work.tile([P, S], F32, name="cosine", tag="cosine", bufs=2)
+            if i == 1:
+                cosine = work.tile([P, S], F32, name="cos_second", tag="cos_second", align_bytes=64)
+            else:
+                cosine = work.tile([P, S], F32, name="cosine", tag="cosine", bufs=2)
             nc.scalar.activation(cosine[:], mag[:], ACT.Sin, bias=half_pi[:], scale=-1.0)
-            prod = work.tile([P, S], F32, name="prod", tag="prod", bufs=2)
+            if i == 1:
+                prod = work.tile([P, S], F32, name="h_first", tag="h_first", align_bytes=64)
+            else:
+                prod = work.tile([P, S], F32, name="prod", tag="prod", bufs=2)
             nc.vector.tensor_tensor(prod[:], a_ps[:], cosine[:], ALU.mult)
-            tag = {4: "h_mid", 7: "h_end"}.get(i, "w1_last" if i % 2 else "h")
+            return prod
+
+        def add_resid(i, prod):
+            ch, c = divmod(i, CHUNK // P)
+            tag = {0: "h_first", 1: "w1_last1", 3: "w1_last0", 5: "w1_last1", 7: "h_end"}.get(i, "h")
             h = work.tile([P, S], F32, name=tag, tag=tag, align_bytes=64)
             nc.vector.tensor_tensor(h[:], prod[:], resids[ch][:, c, :], ALU.add)
             return h
@@ -194,9 +223,10 @@ def tile_list_gazetteer_rival_scores_kernel(
 
         def turn(i):
             b, c = divmod(i, PACK)
-            for half, tag in enumerate((f"d{(i + 1) % 2}", f"a{(i + 1) % 2}")):
+            tags = (f"t{2 * (i % 2)}", f"t{2 * (i % 2) + 1}") if b == 0 else (f"d{(i + 1) % 2}", f"a{(i + 1) % 2}")
+            for half, tag in enumerate(tags):
                 if c == 0:
-                    turned[b, half] = work.tile([P, 4, 2, 4, 64], BF16, name=f"turned{b}{half}")
+                    turned[b, half] = work.tile([P, 4, 2, 4, 64], BF16, name=f"turned{b}{half}", tag=f"turned{b}{half}")
                 ps = bank(tag)
                 for k in range(4):
                     n0 = half * BANK + k * P
@@ -208,12 +238,13 @@ def tile_list_gazetteer_rival_scores_kernel(
 
         page_codes, page_sc = {}, {}
 
-        def quantise_page(b):
-            tag = "h_mid" if b == 0 else "page_codes"
-            both = work.tile([P, HALVES, BANK], U32, name=tag, tag=tag, align_bytes=64)
+        page_bf = {}
+
+        def turn_back(b):
             for half in range(HALVES):
                 words = turned[b, half][:].rearrange("n k u c w -> n (k u c w)").bitcast(F32)
-                grouped = work.tile([P, BANK * PACK], BF16, name="page_bf", tag="page_bf", bufs=2, align_bytes=64)
+                grouped = work.tile([P, BANK * PACK], BF16, name=f"page_bf{b}{half}", align_bytes=64)
+                page_bf[b, half] = grouped
                 pairs = grouped[:].bitcast(F32).rearrange("p (g k n u) -> p g k n u", g=2, k=2, u=2)
                 for g in range(2):
                     ps = bank(f"t{2 * half + g}")
@@ -221,31 +252,45 @@ def tile_list_gazetteer_rival_scores_kernel(
                         w0 = (4 * g + ku) * P
                         nc.tensor.transpose(ps[:, ku * P : (ku + 1) * P], words[:, w0 : w0 + P], ident[:])
                     nc.scalar.copy(pairs[:, g], ps[:].rearrange("p (k u n) -> p k n u", k=2, u=2))
+
+        def quantise_page(b):
+            tag = f"page{R_TILES - 1}" if b == 0 else "page_codes"
+            both = work.tile([P, HALVES, BANK], U32, name=tag, tag=tag, align_bytes=64)
+            for half in range(HALVES):
+                grouped = page_bf[b, half]
                 codes = both[:, half, :]
                 sc = keep.tile([P, BANK], U8, name=f"page_sc{b}{half}", align_bytes=64)
                 nc.vector.quantize_mx(out=codes.bitcast(FP8X4), scales=sc[:], in_=grouped[:])
                 page_codes[b, half], page_sc[b, half] = codes, sc
 
-        h_now = features(0)
+        h_now = add_resid(0, features(0))
         for i in range(R_TILES):
-            ch = i // 2
-            if i % 2 == 0 and ch + 1 < CHUNKS:
-                if ch > 0:
-                    raws[ch + 1] = load_w1(ch + 1)
-                    pages[i + 1] = load_page(i + 1)
-                resids[ch + 1] = load_resid(ch + 1)
-                pages[i + 2] = load_page(i + 2)
-                quantise_w1(ch + 1, raws[ch + 1])
             if i == R_TILES - 2:
                 l_offs2 = load_list(offs2, "l_offs2")
+                for quad in range(4):
+                    nc.sync.dma_start(
+                        tab2_sc[:].bitcast(I32)[32 * quad : 32 * quad + 4 * R_PASSES, :],
+                        tab2_scales.bitcast(I32)[:, 4 * quad : 4 * quad + 4, :],
+                    )
                 tab2_w = [load_words(tab2_words[b], f"tab_w{b}") for b in range(R_PASSES)]
                 pages[i + 1] = load_page(i + 1)
+            ahead = i > 0 and i % 2 == 0
+            if ahead:
+                prod_next = features(i + 1)
             place(i, h_now)
+            if not ahead and i + 1 < R_TILES:
+                prod_next = features(i + 1)
+            if i in (0, 2, 4):
+                quantise_w1(i // 2 + 1, raws[i // 2 + 1])
             if i + 1 < R_TILES:
-                h_now = features(i + 1)
-            turn(i)
-            if i == PACK:
-                quantise_page(0)
+                h_now = add_resid(i + 1, prod_next)
+            if i == 4:
+                for early in range(4):
+                    turn(early)
+            if i >= 4:
+                turn(i)
+            if i == 5:
+                turn_back(0)
 
         l_pos1 = load_list(pos1, "l_pos1")
         l_pos2 = load_list(pos2, "l_pos2")
@@ -256,11 +301,20 @@ def tile_list_gazetteer_rival_scores_kernel(
         v2_w = work.tile([P, R_PASSES, S2], U32, name="v2_w", tag="h_end", align_bytes=64)
         for b in range(R_PASSES):
             nc.vector.tensor_copy(v2_w[:, b, :], tab2_w[b][:].indirect(l_offs2[:]))
-        quantise_page(R_PASSES - 1)
+        quantise_page(0)
+        turn_back(1)
+        quantise_page(1)
+
+        def store(m, capped, second):
+            result = work.tile([P, NP], F32, name="result", tag="result", bufs=2)
+            nc.vector.tensor_tensor(result[:], capped[:], second[:], ALU.min)
+            nc.sync.dma_start(out[m * P : (m + 1) * P, :], result[:])
+
+        pending = None
 
         for m in range(M_TILES):
             cols = slice(m * P, (m + 1) * P)
-            scores = work.tile([P, T2], F32, name="scores", tag="scores", bufs=3)
+            scores = work.tile([P, T2], F32, name="scores", tag="scores", bufs=2)
             for half in range(HALVES):
                 ps = bank(("d", "a")[half] + str((m + 1) % 2))
                 for b in range(R_PASSES):
@@ -270,12 +324,13 @@ def tile_list_gazetteer_rival_scores_kernel(
                         start=(b == 0), stop=(b == R_PASSES - 1),
                     )
                 nc.scalar.copy(scores[:, half * BANK : (half + 1) * BANK], ps[:])
-            first = work.tile([P, NP], F32, name="first", tag="first", bufs=2)
+            first = work.tile([P, NP], F32, name="first", tag="mag", bufs=2)
             nc.vector.tensor_copy(first[:], scores[:].indirect(l_pos1[:]))
-            second = work.tile([P, NP], F32, name="second", tag="second", bufs=2)
+            if pending:
+                store(*pending)
+            second = work.tile([P, NP], F32, name="second", tag="cosine", bufs=2)
             nc.vector.tensor_copy(second[:], scores[:].indirect(l_pos2[:]))
-            capped = work.tile([P, NP], F32, name="capped", tag="capped", bufs=2)
+            capped = work.tile([P, NP], F32, name="capped", tag="prod", bufs=2)
             nc.vector.tensor_tensor(capped[:], first[:], acc_sb[:, m, :], ALU.min)
-            result = work.tile([P, NP], F32, name="result", tag="result", bufs=2)
-            nc.vector.tensor_tensor(result[:], capped[:], second[:], ALU.min)
-            nc.sync.dma_start(out[cols, :], result[:])
+            pending = (m, capped, second)
+        store(*pending)

import math
from contextlib import ExitStack

import concourse.mybir as mybir
from concourse.masks import make_identity

K, T, S, H, T3, S2, T2, NP = 1536, 2048, 512, 1024, 2048, 512, 1024, 512
FLOPS = 2 * (2 * K * H * S + H * S2 * T2)

F32 = mybir.dt.float32
BF16 = mybir.dt.bfloat16
I32 = mybir.dt.int32
U32 = mybir.dt.uint32
U16 = mybir.dt.uint16
U8 = mybir.dt.uint8
FP8X4 = mybir.dt.float8_e4m3fn_x4
FP4X4 = mybir.dt.float4_e2m1fn_x4
ALU = mybir.AluOpType
ACT = mybir.ActivationFunctionType

P = 128
PACK = 4
KP = P * PACK
K_PASSES = K // KP
R_PASSES = H // KP
R_TILES = H // P
M_TILES = S2 // P
CHUNK = 256
CHUNKS = H // CHUNK
BANK = 512
HALVES = T2 // BANK


def tile_list_gazetteer_rival_scores_kernel(
    tc, tab_words, tab_scales, offs, w1, w4_words, w4_scales, bias, resid, page0, wgs,
    tab2_words, tab2_scales, offs2, offs3, pos1, pos2, acc, out,
):
    nc = tc.nc
    with ExitStack() as ctx:
        keep = ctx.enter_context(tc.tile_pool(name="keep", bufs=1))
        work = ctx.enter_context(tc.tile_pool(name="work", bufs=1))
        psum = ctx.enter_context(tc.psum_pool(name="psum", bufs=1))

        def bank(tag):
            return psum.tile([P, BANK], F32, name=tag, tag=tag)

        def load_list(src, name):
            t = keep.tile([P, S // 16], U16, name=name)
            nc.sync.dma_start(t[:], src)
            return t

        def scale_tile(passes, width, name):
            t = keep.tile([P, passes, width], U8, name=name, align_bytes=64)
            nc.vector.memset(t[:].bitcast(I32), 0)
            return t

        def load_scale_rows(t, src):
            words = t[:].bitcast(I32)
            rows = src.bitcast(I32).rearrange("a (q r) w -> r q a w", r=4)
            for r in range(4):
                nc.sync.dma_start(words[r:P:32], rows[r])

        def load_words(src, name):
            t = work.tile([P, T], U32, name=name, tag=name)
            nc.sync.dma_start(t[:].bitcast(I32), src.rearrange("p t i -> p (t i)").bitcast(I32))
            return t

        def gather(window, lst, dtype, name):
            t = keep.tile([P, S], dtype, name=name, align_bytes=64)
            nc.vector.tensor_copy(t[:], window.indirect(lst[:]))
            return t

        tab_sc = scale_tile(K_PASSES, T, "tab_sc")
        w4_sc = scale_tile(K_PASSES, H, "w4_sc")
        ident = keep.tile([P, P], F32, name="ident")
        make_identity(nc, ident[:])
        half_pi = keep.tile([P, 1], F32, name="half_pi")
        zero = keep.tile([P, 1], F32, name="zero")
        nc.vector.memset(zero[:], 0.0)
        nc.vector.tensor_scalar_add(half_pi[:], zero[:], math.pi / 2)
        warm = keep.tile([P, 1], F32, name="warm")
        nc.scalar.activation(warm[:], zero[:], ACT.Sin, bias=zero[:])
        bias_rows = keep.tile([P, P], F32, name="bias_rows")
        nc.vector.memset(bias_rows[:], 0.0)
        tab2_sc = keep.tile([P, T3], U8, name="tab2_sc", align_bytes=64)
        nc.vector.memset(tab2_sc[:].bitcast(I32), 0)

        l_offs = load_list(offs, "l_offs")

        w1_codes, w1_sc = {}, {}

        def load_w1(ch):
            raws = []
            for a in range(K_PASSES):
                if ch == CHUNKS - 1 and a > 0:
                    raw = work.tile([P, PACK, CHUNK], F32, name=f"turned0{a - 1}", tag=f"turned0{a - 1}")
                else:
                    raw = work.tile([P, PACK, CHUNK], F32, name="w1_raw", tag="w1_raw", bufs=6)
                nc.sync.dma_start(
                    raw[:],
                    w1[a * KP : (a + 1) * KP, ch * CHUNK : (ch + 1) * CHUNK].rearrange("(p j) c -> p j c", j=PACK),
                )
                raws.append(raw)
            return raws

        def quantise_w1(ch, raws):
            tag = "cos_second" if ch == 1 else f"w1_codes{ch}"
            codes = work.tile([P, K_PASSES, CHUNK], U32, name=tag, tag=tag, align_bytes=64)
            sc = keep.tile([P, K_PASSES, CHUNK], U8, name=f"w1_sc{ch}", align_bytes=64)
            for a in range(K_PASSES):
                tag = f"w1_last{ch % 2}" if a == K_PASSES - 1 else f"w1_bf{a}{ch % 2}"
                grouped = work.tile([P, CHUNK, PACK], BF16, name=tag, tag=tag, align_bytes=64)
                round_copy = nc.vector.tensor_copy if ch == 0 else nc.scalar.copy
                round_copy(
                    grouped[:].rearrange("p (c i) t -> p c t i", i=4),
                    raws[a][:].rearrange("p t (c i) -> p c t i", i=4),
                )
                nc.vector.quantize_mx(
                    out=codes[:, a, :].bitcast(FP8X4), scales=sc[:, a, :],
                    in_=grouped[:].rearrange("p c t -> p (c t)"),
                )
            w1_codes[ch], w1_sc[ch] = codes, sc

        def load_w4(c0, c1, name):
            t = keep.tile([P, K_PASSES, 2 * (c1 - c0)], U8, name=name, align_bytes=64)
            nc.sync.dma_start(
                t[:].bitcast(I32),
                w4_words.bitcast(I32)[:, :, c0 // 2 : c1 // 2].rearrange("a p w -> p a w"),
            )
            return t

        def load_resid(ch):
            t = keep.tile([P, 2, S], F32, name=f"resid{ch}")
            nc.sync.dma_start(t[:], resid[ch * CHUNK : (ch + 1) * CHUNK, :].rearrange("(c q) j -> q c j", q=P))
            return t

        def load_page(i):
            t = work.tile([P, T2], F32, name=f"page{i}", tag=f"page{i}", align_bytes=64)
            nc.sync.dma_start(t[:], page0[i * P : (i + 1) * P, :])
            return t

        w4_first = load_w4(0, CHUNK, "w4_first")
        tab_w = [load_words(tab_words[0], "tab_w0")]
        load_scale_rows(tab_sc, tab_scales)
        tab_w.append(load_words(tab_words[1], "tab_w1"))
        load_scale_rows(w4_sc, w4_scales)
        nc.sync.dma_start(bias_rows[0:R_TILES, :], bias.rearrange("(c q) -> c q", q=P))
        tab_w.append(load_words(tab_words[2], "tab_w2"))
        raws = {0: load_w1(0)}
        l_offs3 = load_list(offs3, "l_offs3")
        resids = {0: load_resid(0)}
        wgs_sb = work.tile([P, S], F32, name="wgs_sb", tag="wgs_sb", align_bytes=64)
        nc.sync.dma_start(wgs_sb[:], wgs)
        pages = {0: load_page(0)}
        raws[1] = load_w1(1)
        pages[1] = load_page(1)
        w4_rest = load_w4(CHUNK, H, "w4_rest")
        resids[1] = load_resid(1)
        pages[2] = load_page(2)
        raws[2] = load_w1(2)
        pages[3] = load_page(3)
        raws[3] = load_w1(3)
        resids[2] = load_resid(2)
        pages[4] = load_page(4)
        pages[5] = load_page(5)
        resids[3] = load_resid(3)
        pages[6] = load_page(6)

        bias_ps = bank("t0")
        nc.tensor.transpose(bias_ps[:, 0:P], bias_rows[:], ident[:])
        bias_sb = keep.tile([P, R_TILES], F32, name="bias_sb")
        nc.scalar.copy(bias_sb[:], bias_ps[:, 0:R_TILES])

        v_sc = [gather(tab_sc[:, a, :], l_offs, U8, f"v_sc{a}") for a in range(K_PASSES)]
        v_w = [gather(tab_w[a][:], l_offs, U32, f"v_w{a}") for a in range(K_PASSES)]
        quantise_w1(0, raws[0])

        def features(i):
            ch, c = divmod(i, CHUNK // P)
            side = 0 if i == 1 else i % 2
            d_ps = bank(f"d{side}")
            a_ps = bank(f"a{side}")
            w4_t, c0 = (w4_first, i * P) if ch == 0 else (w4_rest, i * P - CHUNK)
            for a in range(K_PASSES):
                nc.tensor.matmul_mx(
                    out=d_ps[:], lhsT=w4_t[:, a, 2 * c0 : 2 * (c0 + P)].bitcast(FP4X4),
                    lhsT_scale=w4_sc[:, a, i * P : (i + 1) * P],
                    rhs=v_w[a][:].bitcast(FP8X4), rhs_scale=v_sc[a][:],
                    start=(a == 0), stop=(a == K_PASSES - 1),
                )
            for a in range(K_PASSES):
                nc.tensor.matmul_mx(
                    out=a_ps[:], lhsT=w1_codes[ch][:, a, c * P : (c + 1) * P].bitcast(FP8X4),
                    lhsT_scale=w1_sc[ch][:, a, c * P : (c + 1) * P],
                    rhs=v_w[a][:].bitcast(FP8X4), rhs_scale=v_sc[a][:],
                    start=(a == 0), stop=(a == K_PASSES - 1),
                )
            mag = work.tile([P, S], F32, name="mag", tag="mag", bufs=2)
            nc.scalar.activation(mag[:], d_ps[:], ACT.Abs, bias=bias_sb[:, i : i + 1])
            if i == 1:
                cosine = work.tile([P, S], F32, name="cos_second", tag="cos_second", align_bytes=64)
            else:
                cosine = work.tile([P, S], F32, name="cosine", tag="cosine", bufs=2)
            nc.scalar.activation(cosine[:], mag[:], ACT.Sin, bias=half_pi[:], scale=-1.0)
            if i == 1:
                prod = work.tile([P, S], F32, name="h_first", tag="h_first", align_bytes=64)
            else:
                prod = work.tile([P, S], F32, name="prod", tag="prod", bufs=2)
            nc.vector.tensor_tensor(prod[:], a_ps[:], cosine[:], ALU.mult)
            return prod

        def add_resid(i, prod):
            ch, c = divmod(i, CHUNK // P)
            tag = {0: "h_first", 1: "w1_last1", 3: "w1_last0", 5: "w1_last1", 7: "h_end"}.get(i, "h")
            h = work.tile([P, S], F32, name=tag, tag=tag, align_bytes=64)
            nc.vector.tensor_tensor(h[:], prod[:], resids[ch][:, c, :], ALU.add)
            return h

        turned = {}

        def place(i, h):
            nc.vector.tensor_tensor(pages[i][:].indirect(l_offs3[:]), h[:], wgs_sb[:], ALU.mult)

        def turn(i):
            b, c = divmod(i, PACK)
            tags = (f"t{2 * (i % 2)}", f"t{2 * (i % 2) + 1}") if b == 0 else (f"d{(i + 1) % 2}", f"a{(i + 1) % 2}")
            for half, tag in enumerate(tags):
                if c == 0:
                    turned[b, half] = work.tile([P, 4, 2, 4, 64], BF16, name=f"turned{b}{half}", tag=f"turned{b}{half}")
                ps = bank(tag)
                for k in range(4):
                    n0 = half * BANK + k * P
                    nc.tensor.transpose(ps[:, k * P : (k + 1) * P], pages[i][:, n0 : n0 + P], ident[:])
                nc.scalar.copy(
                    turned[b, half][:, :, :, c, :].rearrange("n k u (p e) -> n k u p e", e=2),
                    ps[:].rearrange("n (k p u e) -> n k u p e", k=4, u=2, e=2),
                )

        page_codes, page_sc = {}, {}

        page_bf = {}

        def turn_back(b):
            for half in range(HALVES):
                words = turned[b, half][:].rearrange("n k u c w -> n (k u c w)").bitcast(F32)
                grouped = work.tile([P, BANK * PACK], BF16, name=f"page_bf{b}{half}", align_bytes=64)
                page_bf[b, half] = grouped
                pairs = grouped[:].bitcast(F32).rearrange("p (g k n u) -> p g k n u", g=2, k=2, u=2)
                for g in range(2):
                    ps = bank(f"t{2 * half + g}")
                    for ku in range(4):
                        w0 = (4 * g + ku) * P
                        nc.tensor.transpose(ps[:, ku * P : (ku + 1) * P], words[:, w0 : w0 + P], ident[:])
                    nc.scalar.copy(pairs[:, g], ps[:].rearrange("p (k u n) -> p k n u", k=2, u=2))

        def quantise_page(b):
            tag = f"page{R_TILES - 1}" if b == 0 else "page_codes"
            both = work.tile([P, HALVES, BANK], U32, name=tag, tag=tag, align_bytes=64)
            for half in range(HALVES):
                grouped = page_bf[b, half]
                codes = both[:, half, :]
                sc = keep.tile([P, BANK], U8, name=f"page_sc{b}{half}", align_bytes=64)
                nc.vector.quantize_mx(out=codes.bitcast(FP8X4), scales=sc[:], in_=grouped[:])
                page_codes[b, half], page_sc[b, half] = codes, sc

        h_now = add_resid(0, features(0))
        for i in range(R_TILES):
            if i == R_TILES - 2:
                l_offs2 = load_list(offs2, "l_offs2")
                for quad in range(4):
                    nc.sync.dma_start(
                        tab2_sc[:].bitcast(I32)[32 * quad : 32 * quad + 4 * R_PASSES, :],
                        tab2_scales.bitcast(I32)[:, 4 * quad : 4 * quad + 4, :],
                    )
                tab2_w = [load_words(tab2_words[b], f"tab_w{b}") for b in range(R_PASSES)]
                pages[i + 1] = load_page(i + 1)
            ahead = i > 0 and i % 2 == 0
            if ahead:
                prod_next = features(i + 1)
            place(i, h_now)
            if not ahead and i + 1 < R_TILES:
                prod_next = features(i + 1)
            if i in (0, 2, 4):
                quantise_w1(i // 2 + 1, raws[i // 2 + 1])
            if i + 1 < R_TILES:
                h_now = add_resid(i + 1, prod_next)
            if i == 4:
                for early in range(4):
                    turn(early)
            if i >= 4:
                turn(i)
            if i == 5:
                turn_back(0)

        l_pos1 = load_list(pos1, "l_pos1")
        l_pos2 = load_list(pos2, "l_pos2")
        acc_sb = keep.tile([P, M_TILES, NP], F32, name="acc_sb")
        nc.sync.dma_start(acc_sb[:], acc.rearrange("(m q) j -> q m j", q=P))
        v2_sc = work.tile([P, S2], U8, name="v2_sc", tag="wgs_sb", align_bytes=64)
        nc.vector.tensor_copy(v2_sc[:], tab2_sc[:].indirect(l_offs2[:]))
        v2_w = work.tile([P, R_PASSES, S2], U32, name="v2_w", tag="h_end", align_bytes=64)
        for b in range(R_PASSES):
            nc.vector.tensor_copy(v2_w[:, b, :], tab2_w[b][:].indirect(l_offs2[:]))
        quantise_page(0)
        turn_back(1)
        quantise_page(1)

        def store(m, capped, second):
            result = work.tile([P, NP], F32, name="result", tag="result", bufs=2)
            nc.vector.tensor_tensor(result[:], capped[:], second[:], ALU.min)
            nc.sync.dma_start(out[m * P : (m + 1) * P, :], result[:])

        pending = None

        for m in range(M_TILES):
            cols = slice(m * P, (m + 1) * P)
            scores = work.tile([P, T2], F32, name="scores", tag="scores", bufs=2)
            for half in range(HALVES):
                ps = bank(("d", "a")[half] + str((m + 1) % 2))
                for b in range(R_PASSES):
                    nc.tensor.matmul_mx(
                        out=ps[:], lhsT=v2_w[:, b, cols].bitcast(FP8X4), lhsT_scale=v2_sc[4 * b : P, cols],
                        rhs=page_codes[b, half].bitcast(FP8X4), rhs_scale=page_sc[b, half][:],
                        start=(b == 0), stop=(b == R_PASSES - 1),
                    )
                nc.scalar.copy(scores[:, half * BANK : (half + 1) * BANK], ps[:])
            first = work.tile([P, NP], F32, name="first", tag="mag", bufs=2)
            nc.vector.tensor_copy(first[:], scores[:].indirect(l_pos1[:]))
            if pending:
                store(*pending)
            second = work.tile([P, NP], F32, name="second", tag="cosine", bufs=2)
            nc.vector.tensor_copy(second[:], scores[:].indirect(l_pos2[:]))
            capped = work.tile([P, NP], F32, name="capped", tag="prod", bufs=2)
            nc.vector.tensor_tensor(capped[:], first[:], acc_sb[:, m, :], ALU.min)
            pending = (m, capped, second)
        store(*pending)
